import numpy as np
import ml_dtypes


def mxq(x, axis, fmt="e4m3"):
    dtype, down = {"e4m3": (ml_dtypes.float8_e4m3fn, 7), "e5m2": (ml_dtypes.float8_e5m2, 14)}[fmt]
    v = np.moveaxis(np.asarray(x, np.float32).astype(ml_dtypes.bfloat16).astype(np.float64), axis, -1)
    blocks = v.reshape(v.shape[:-1] + (-1, 32))
    amax = np.abs(blocks).max(-1, keepdims=True)
    byte = np.maximum(np.where(amax > 0, np.frexp(amax)[1] - 1 + 127, 0) - down, 1)
    scale = np.exp2(byte - 127.0)
    codes = (blocks / scale).astype(np.float32).astype(dtype).astype(np.float64)
    return np.moveaxis((codes * scale).reshape(v.shape), -1, axis)


WIDE = False


def mx_kscale(k):
    if not WIDE:
        return np.ones(k)
    levels = np.array([10, -10, 5, -5, 0])
    if k % 512:
        return np.exp2(np.random.permutation(np.resize(levels, k // 32))).repeat(32)
    a = np.empty((k // 512, 16))
    for p in range(k // 512):
        a[p, :8] = np.random.permutation(np.resize(levels, 8))
        for g in range(8):
            far = levels[np.abs(levels - a[p, g]) >= 10]
            a[p, g + 8] = far[np.random.randint(len(far))]
    return np.exp2(a.ravel()).repeat(32)


BF16 = ml_dtypes.bfloat16


def bf(x):
    return np.asarray(x, np.float32).astype(BF16)


def f64(x):
    return np.asarray(x).astype(np.float64)


E2M1 = np.array([0.0, 0.5, 1.0, 1.5, 2.0, 3.0, 4.0, 6.0, -0.0, -0.5, -1.0, -1.5, -2.0, -3.0, -4.0, -6.0])


def pack_weight(w, fmt):
    k, n = w.shape
    w = f64(bf(w)).reshape(k // 32, 32, n)
    amax = np.abs(w).max(1)
    if fmt == "e4m3":
        byte = np.frexp(amax)[1] - 1 + 127 - 7
    else:
        mant, ex = np.frexp(amax / 6.0)
        byte = np.where(mant > 0.5, ex, ex - 1) + 127
    byte = np.clip(np.where(amax > 0, byte, 1), 1, 254)
    scaled = (w * np.exp2(127.0 - byte)[:, None, :]).reshape(k, n).astype(np.float32)
    by_word = np.ascontiguousarray(scaled.reshape(k // 512, 128, 4, n).transpose(0, 1, 3, 2))
    if fmt == "e4m3":
        words = by_word.astype(ml_dtypes.float8_e4m3fn).view(np.uint8)
    else:
        c = by_word.astype(ml_dtypes.float4_e2m1fn).view(np.uint8) & 0xF
        words = c[..., 0::2] | (c[..., 1::2] << 4)
    return np.ascontiguousarray(words), np.ascontiguousarray(byte.astype(np.uint8).reshape(k // 512, 16, n))


def unpack_weight(words, scales, fmt):
    g, p, n, _ = words.shape
    if fmt == "e4m3":
        vals = np.ascontiguousarray(words).view(ml_dtypes.float8_e4m3fn).astype(np.float64)
    else:
        nib = np.empty((g, p, n, 4), np.uint8)
        nib[..., 0::2] = words & 0xF
        nib[..., 1::2] = words >> 4
        vals = E2M1[nib]
    vals = vals * np.repeat(np.exp2(scales.astype(np.float64) - 127.0), 8, axis=1)[..., None]
    return vals.transpose(0, 1, 3, 2).reshape(g * 512, n)
def pack4(w):
    words, scales = pack_weight(w, "e2m1")
    return words.reshape(words.shape[0], 128, -1), scales


def unpack4(words, scales):
    return unpack_weight(words.reshape(words.shape[0], 128, -1, 2), scales, "e2m1")


def planes(Y):
    n, m = Y.shape
    b = f64(bf(Y)).reshape(n // 32, 32, m)
    amax = np.abs(b).max(1)
    byte = np.clip(np.where(amax > 0, np.frexp(amax)[1] - 1 + 127 - 7, 1), 1, 254)
    codes = (b * np.exp2(127.0 - byte)[:, None, :]).reshape(n, m).astype(np.float32).astype(ml_dtypes.float8_e4m3fn).view(np.uint8)
    words = codes.reshape(n // 512, 128, 4, m).transpose(0, 1, 3, 2)
    return np.ascontiguousarray(words), np.ascontiguousarray(byte.astype(np.uint8).reshape(n // 512, 16, m))


S, T, D, N = 2, 768, 1024, 1024


def setup_inputs():
    t = mx_kscale(D)
    base = np.random.randn(T, D)
    cond = base + 0.5 * np.random.randn(T, D)
    uncond = base + 0.5 * np.random.randn(T, D)
    x = np.concatenate([cond, uncond], axis=0) * t
    guide = 1.5 + 0.5 * np.random.rand(T)
    w1 = np.random.randn(D, D) * (0.5 / np.sqrt(D)) / t[:, None] * t
    w2 = np.random.randn(D, D) * (0.35 / np.sqrt(D)) / t[:, None] * t
    w3 = np.random.randn(D, N) / np.sqrt(D) * np.exp(0.8 * np.random.randn(N)) / t[:, None]
    w1_words, w1_scales = pack4(w1)
    return {"x": bf(x), "guide": bf(guide), "w1_words": w1_words, "w1_scales": w1_scales,
            "w2": bf(w2), "w3": bf(w3)}


def reference(x, guide, w1_words, w1_scales, w2, w3):
    x, guide, w2, w3 = f64(x), f64(guide), f64(w2), f64(w3)
    w1 = unpack4(w1_words, w1_scales)
    h = x + np.maximum(mxq(x, 1, "e4m3") @ w1, 0.0)
    e = h[T:] + guide[:, None] * (h[:T] - h[T:])
    m = e + (mxq(e, 1, "e4m3") @ mxq(w2, 0, "e4m3"))
    y = mxq(m, 1, "e4m3") @ mxq(w3, 0, "e4m3")
    words, scales = planes(y.T)
    return y, words, scales

@@ -1,0 +1,388 @@
+from contextlib import ExitStack
+
+import concourse.mybir as mybir
+from concourse.masks import make_identity
+
+T, D = 768, 1024
+FLOPS = 2 * (2 * T + T + T) * D * D
+
+F32 = mybir.dt.float32
+BF16 = mybir.dt.bfloat16
+I32 = mybir.dt.int32
+U32 = mybir.dt.uint32
+U8 = mybir.dt.uint8
+FP8X4 = mybir.dt.float8_e4m3fn_x4
+FP4X4 = mybir.dt.float4_e2m1fn_x4
+ALU = mybir.AluOpType
+ACT = mybir.ActivationFunctionType
+
+P = 128
+TILES = T // P
+HALF = 512
+BANKS = 8
+
+SCALE_ENG = "SSSS"
+ECAST = "SSVSSS"
+YC = ["VV"] * 5 + ["PP"]
+YE = ["SS"] * 5 + ["SV"]
+YTE = ["SS"] * 5 + ["SV"]
+WSPLIT = 56
+MOVED = {("xq", 1): (-1, 1)}
+XEVAC = "SS"
+EB = 12
+SCHED = "mv:0 w:-1 yT0:9 yT1:9 s10:0 s11:0 H0:0 sc0:0 H1:0 sc1:0 eT0:1 eT1:1 ee0:1 ee1:1 xT:-2 xe:-2 s20:5 s21:5 yte0:9 yte1:9 s30:7 s31:7 xq:-1 w:0 ec:3 M0:5 M1:5 ye0:7 ye1:7 eq:4 yq0:9 yq1:9 w:1 mq:5 yc0:7 yc1:7 w:2 mv:1"
+W_PLAN = [[0,0,"v",0],[0,2,"s",0],[1,0,"q",0],[1,0,"v",2],[1,2,"s",2],[2,0,"q",2],[2,0,"v",1],[2,2,"s",1],[3,0,"q",1],[3,0,"v",3],[3,2,"s",3],[4,0,"q",3],[4,0,"v",4],[4,2,"s",4],[5,0,"q",4],[5,0,"v",5],[5,2,"s",5],[6,-1,"S",6],[6,0,"q",5],[6,0,"V",7],[6,1,"q",7],[6,2,"q",6]]
+LOADS = "x0 x1 w x2 a0 x3 a1 b0 x4 b1 x5"
+
+
+def tile_guided_hidden_noise_head_k1_kernel(tc, x, guide, w1_words, w1_scales, w2, w3, out_0, out_1, out_2):
+    nc = tc.nc
+    with ExitStack() as ctx:
+        keep = ctx.enter_context(tc.tile_pool(name="keep", bufs=1))
+        work = ctx.enter_context(tc.tile_pool(name="work", bufs=2))
+        psum = ctx.enter_context(tc.psum_pool(name="psum", bufs=1))
+        ctx.enter_context(tc.manual_schedule())
+
+        fills = []
+
+        def next_bank():
+            fills.append(len(fills))
+            return psum.tile([P, HALF], F32, name="bank", tag="bank%d" % (fills[-1] % BANKS))
+
+        def copy_on(engine, out, in_):
+            if engine == "S":
+                nc.scalar.copy(out=out, in_=in_)
+            else:
+                nc.vector.tensor_copy(out=out, in_=in_)
+
+        w1_plane = keep.tile([P, 2, D], U8, name="w1_plane", align_bytes=64)
+        nc.vector.memset(w1_plane[:].bitcast(I32), 0)
+        guide_rows = keep.tile([P, P], BF16, name="guide_rows")
+        nc.vector.memset(guide_rows[:], 0.0)
+        warm = keep.tile([P, 2], F32, name="warm")
+        nc.vector.memset(warm[:], 0.0)
+        ident = keep.tile([P, P], F32, name="ident")
+        make_identity(nc, ident[:])
+        nc.scalar.dma_start(out=guide_rows[0:TILES, :], in_=guide.rearrange("(j i) -> j i", i=P))
+        if "S" in SCALE_ENG:
+            nc.scalar.activation(out=warm[:, 1:2], in_=warm[:, 0:1], func=ACT.Copy, scale=1.0)
+
+        x_rows = {}
+        w_raw = {}
+
+        def load_x(j):
+            for b in range(2):
+                x_rows[j, b] = keep.tile([P, D], BF16, name="x_rows%d_%d" % (j, b))
+                nc.sync.dma_start(out=x_rows[j, b][:], in_=x[b * T + j * P : b * T + (j + 1) * P, :])
+
+        def load_w(n):
+            w = w2 if n < 4 else w3
+            g = n % 2
+            raw = keep.tile([P, 4, D], BF16, name="w_raw%d" % n)
+            nc.sync.dma_start(out=raw[:], in_=w[g * HALF : (g + 1) * HALF, :].rearrange("(p j) c -> p j c", j=4))
+            w_raw[n] = raw[:, :, 0:HALF]
+            w_raw[n + 2] = raw[:, :, HALF:D]
+
+        w1_codes = keep.tile([P, 2, 2 * D], U8, name="w1_codes", align_bytes=64)
+
+        def load_w1():
+            for q in range(4):
+                nc.sync.dma_start(
+                    out=w1_plane[32 * q : 32 * q + 4, :, :].bitcast(I32),
+                    in_=w1_scales.bitcast(I32)[:, 4 * q : 4 * q + 4, :].rearrange("g r n -> r g n"),
+                )
+            nc.sync.dma_start(out=w1_codes[:].bitcast(I32), in_=w1_words.bitcast(I32).rearrange("g p n -> p g n"))
+
+        for item in LOADS.split():
+            if item == "w":
+                load_w1()
+            elif item[0] == "x":
+                load_x(int(item[1]))
+            else:
+                load_w(int(item[1]) + (0 if item[0] == "a" else 4))
+
+        guide_f32 = keep.tile([P, P], F32, name="guide_f32")
+        weight = keep.tile([P, 2, 8], F32, name="weight")
+
+        def widen_guide():
+            nc.vector.tensor_copy(out=guide_f32[:], in_=guide_rows[:])
+
+        def make_weights():
+            bank = next_bank()
+            nc.tensor.transpose(bank[:, 0:P], guide_f32[:], ident[:])
+            nc.vector.tensor_copy(out=weight[:, 0, :], in_=bank[:, 0:8])
+            nc.vector.tensor_scalar(out=weight[:, 1, :], in0=bank[:, 0:8], scalar1=-1.0, scalar2=1.0, op0=ALU.mult, op1=ALU.add)
+
+        w_codes = {}
+        w_plane = {}
+        w_grouped = {}
+
+        def group_w(n, engine):
+            if n not in w_grouped:
+                w_grouped[n] = work.tile([P, 4 * HALF], BF16, name="w_grouped", bufs=3, align_bytes=64)
+            lo, hi = {"V": (0, 64), "S": (0, 64), "v": (0, WSPLIT), "s": (WSPLIT, 64)}[engine]
+            if n < 4:
+                copy_on(
+                    engine.replace("v", "V").replace("s", "S"),
+                    w_grouped[n][:].rearrange("p (t c m j) -> p c t m j", t=4, m=2, j=4)[:, lo:hi],
+                    w_raw[n].rearrange("p j (c m t) -> p c t m j", m=2, t=4)[:, lo:hi],
+                )
+            else:
+                copy_on(
+                    engine.replace("v", "V").replace("s", "S"),
+                    w_grouped[n][:].rearrange("p (c i j) -> p c j i", i=4, j=4)[:, 2 * lo : 2 * hi],
+                    w_raw[n].rearrange("p j (c i) -> p c j i", i=4)[:, 2 * lo : 2 * hi],
+                )
+
+        def quantize_w(n):
+            w_codes[n] = keep.tile([P, HALF], U32, name="w_codes%d" % n, align_bytes=64)
+            w_plane[n] = keep.tile([P, HALF], U8, name="w_plane%d" % n, align_bytes=64)
+            nc.vector.quantize_mx(out=w_codes[n][:].bitcast(FP8X4), scales=w_plane[n][:], in_=w_grouped[n][:])
+
+        tiles = {}
+
+        def quantize(kind, j, width):
+            codes = work.tile([P, width // 4], U32, name=kind + "_codes", bufs=4, align_bytes=64)
+            plane = work.tile([P, width // 4], U8, name=kind + "_plane", bufs=4, align_bytes=64)
+            nc.vector.quantize_mx(out=codes[:].bitcast(FP8X4), scales=plane[:], in_=tiles[kind + "_grouped", j][:])
+            tiles[kind + "_codes", j] = codes
+            tiles[kind + "_plane", j] = plane
+
+        def transpose_x(j):
+            for b in range(2):
+                words = x_rows[j, b][:].bitcast(F32)
+                bank = next_bank()
+                tiles["x_bank", j, b] = bank
+                for g in range(2):
+                    for u in range(2):
+                        nc.tensor.transpose(
+                            bank[:, (2 * g + u) * P : (2 * g + u + 1) * P], words[:, 256 * g + u : 256 * (g + 1) : 2], ident[:]
+                        )
+
+        def group_x(j):
+            grouped = work.tile([P, 2 * D], BF16, name="x_grouped", bufs=3, align_bytes=64)
+            tiles["x_grouped", j] = grouped
+            for b in range(2):
+                copy_on(
+                    XEVAC[b],
+                    grouped[:, b * D : (b + 1) * D].bitcast(F32).rearrange("p (g r u) -> p g r u", g=2, u=2),
+                    tiles["x_bank", j, b][:].rearrange("p (g u r) -> p g r u", g=2, u=2),
+                )
+
+        def quantize_x(j):
+            quantize("x", j, 2 * D)
+
+        def stage1(j, h):
+            codes, plane = tiles["x_codes", j], tiles["x_plane", j]
+            for b in range(2):
+                bank = next_bank()
+                tiles["h_bank", j, h, b] = bank
+                for g in range(2):
+                    cols = slice((2 * b + g) * P, (2 * b + g + 1) * P)
+                    nc.tensor.matmul_mx(
+                        out=bank[:],
+                        lhsT=codes[:, cols].bitcast(FP8X4),
+                        lhsT_scale=plane[:, cols],
+                        rhs=w1_codes[:, g, 2 * h * HALF : 2 * (h + 1) * HALF].bitcast(FP4X4),
+                        rhs_scale=w1_plane[:, g, h * HALF : (h + 1) * HALF],
+                        start=(g == 0),
+                        stop=(g == 1),
+                    )
+
+        def residual(j, h):
+            for b in range(2):
+                hidden = work.tile([P, HALF], F32, name="hidden", bufs=6)
+                tiles["hidden", j, h, b] = hidden
+                nc.vector.scalar_tensor_tensor(
+                    out=hidden[:].rearrange("p (t m) -> p t m", t=4),
+                    in0=tiles["h_bank", j, h, b][:].rearrange("p (m t) -> p t m", t=4),
+                    scalar=0.0,
+                    in1=x_rows[j, b][:, h * HALF : (h + 1) * HALF].rearrange("p (m t) -> p t m", t=4),
+                    op0=ALU.max,
+                    op1=ALU.add,
+                )
+
+        def weigh(j, h):
+            for b in range(2):
+                term = work.tile([P, HALF], F32, name="term", bufs=8)
+                tiles["term", j, h, b] = term
+                hidden = tiles["hidden", j, h, b]
+                factor = weight[:, b, j : j + 1]
+                engine = SCALE_ENG[2 * h + b]
+                if engine == "S":
+                    nc.scalar.activation(out=term[:], in_=hidden[:], func=ACT.Copy, scale=factor)
+                elif engine == "G":
+                    nc.gpsimd.tensor_scalar(out=term[:], in0=hidden[:], scalar1=factor, scalar2=0.0, op0=ALU.mult, op1=ALU.add)
+                else:
+                    nc.vector.tensor_scalar(out=term[:], in0=hidden[:], scalar1=factor, scalar2=None, op0=ALU.mult)
+
+        def transpose_e(j, h):
+            bank = next_bank()
+            tiles["e_bank", j, h] = bank
+            for t in range(4):
+                for b in range(2):
+                    nc.tensor.matmul(
+                        bank[:, t * P : (t + 1) * P],
+                        lhsT=tiles["term", j, h, b][:, t * P : (t + 1) * P],
+                        rhs=ident[:],
+                        start=(b == 0),
+                        stop=(b == 1),
+                        is_transpose=True,
+                    )
+
+        def keep_e(j, h):
+            bank = tiles["e_bank", j, h]
+            exact = work.tile([P, HALF], F32, name="e_exact", bufs=EB)
+            tiles["e_exact", j, h] = exact
+            nc.scalar.copy(out=exact[:].rearrange("p (n t) -> p n t", t=4), in_=bank[:].rearrange("p (t n) -> p n t", t=4))
+
+        def round_e(j):
+            tiles["e_grouped", j] = work.tile([P, D], BF16, name="e_grouped", bufs=3, align_bytes=64)
+            for h in range(2):
+                dst = tiles["e_grouped", j][:, h * HALF : (h + 1) * HALF]
+                if ECAST[j] == "V":
+                    nc.vector.tensor_copy(out=dst, in_=tiles["e_exact", j, h][:])
+                else:
+                    nc.scalar.copy(out=dst, in_=tiles["e_exact", j, h][:])
+
+        def quantize_e(j):
+            quantize("e", j, D)
+
+        def stage2(j, h):
+            codes, plane = tiles["e_codes", j], tiles["e_plane", j]
+            bank = next_bank()
+            tiles["m_bank", j, h] = bank
+            for t in range(4):
+                for g in range(2):
+                    nc.tensor.matmul_mx(
+                        out=bank[:, t * P : (t + 1) * P],
+                        lhsT=w_codes[2 * h + g][:, t * P : (t + 1) * P].bitcast(FP8X4),
+                        lhsT_scale=w_plane[2 * h + g][:, t * P : (t + 1) * P],
+                        rhs=codes[:, g * P : (g + 1) * P].bitcast(FP8X4),
+                        rhs_scale=plane[:, g * P : (g + 1) * P],
+                        start=(g == 0),
+                        stop=(g == 1),
+                    )
+
+        def mix(j, h):
+            if h == 0:
+                tiles["m_grouped", j] = work.tile([P, D], BF16, name="m_grouped", bufs=3, align_bytes=64)
+            nc.vector.tensor_tensor(
+                out=tiles["m_grouped", j][:, h * HALF : (h + 1) * HALF].rearrange("p (n t) -> p n t", t=4),
+                in0=tiles["m_bank", j, h][:].rearrange("p (t n) -> p n t", t=4),
+                in1=tiles["e_exact", j, h][:].rearrange("p (n t) -> p n t", t=4),
+                op=ALU.add,
+            )
+
+        def quantize_m(j):
+            quantize("m", j, D)
+
+        def stage3(j, h):
+            codes, plane = tiles["m_codes", j], tiles["m_plane", j]
+            bank = next_bank()
+            tiles["y_bank", j, h] = bank
+            for g in range(2):
+                nc.tensor.matmul_mx(
+                    out=bank[:],
+                    lhsT=codes[:, g * P : (g + 1) * P].bitcast(FP8X4),
+                    lhsT_scale=plane[:, g * P : (g + 1) * P],
+                    rhs=w_codes[4 + 2 * h + g][:].bitcast(FP8X4),
+                    rhs_scale=w_plane[4 + 2 * h + g][:],
+                    start=(g == 0),
+                    stop=(g == 1),
+                )
+
+        def store_y(j, h):
+            bank = tiles["y_bank", j, h]
+            result = work.tile([P, HALF], F32, name="result", bufs=6)
+            rounded = work.tile([P, HALF], BF16, name="y_rounded", bufs=6)
+            tiles["result", j, h] = result
+            tiles["y_rounded", j, h] = rounded
+            if YC[j][h] == "P":
+                copy_on(
+                    YE[j][h],
+                    rounded[:].rearrange("p (u m e) -> p u m e", u=2, e=2),
+                    bank[:].rearrange("p (m u e) -> p u m e", u=2, e=2),
+                )
+            copy_on(YE[j][h], result[:], bank[:])
+            nc.sync.dma_start(out=out_0[j * P : (j + 1) * P, h * HALF : (h + 1) * HALF], in_=result[:])
+
+        def round_y(j, h):
+            if YC[j][h] != "P":
+                copy_on(
+                    YC[j][h],
+                    tiles["y_rounded", j, h][:].rearrange("p (u m e) -> p u m e", u=2, e=2),
+                    tiles["result", j, h][:].rearrange("p (m u e) -> p u m e", u=2, e=2),
+                )
+
+        def transpose_y(j, h):
+            words = tiles["y_rounded", j, h][:].bitcast(F32)
+            bank = next_bank()
+            tiles["t_bank", j, h] = bank
+            for u in range(2):
+                nc.tensor.transpose(bank[:, u * P : (u + 1) * P], words[:, u * P : (u + 1) * P], ident[:])
+
+        def group_y(j, h):
+            grouped = work.tile([P, HALF], BF16, name="y_grouped", bufs=4, align_bytes=64)
+            tiles["y_grouped", j, h] = grouped
+            copy_on(
+                YTE[j][h],
+                grouped[:].bitcast(F32).rearrange("p (r u) -> p r u", u=2),
+                tiles["t_bank", j, h][:, 0 : 2 * P].rearrange("p (u r) -> p r u", u=2),
+            )
+
+        y_plane = keep.tile([P, 2, T], U8, name="y_plane", align_bytes=64)
+
+        def quantize_y(j, h):
+            codes = work.tile([P, P], U32, name="y_codes", bufs=6, align_bytes=64)
+            nc.vector.quantize_mx(
+                out=codes[:].bitcast(FP8X4),
+                scales=y_plane[:, h, j * P : (j + 1) * P],
+                in_=tiles["y_grouped", j, h][:],
+            )
+            nc.sync.dma_start(
+                out=out_1[h, :, j * P : (j + 1) * P, :].rearrange("p m t -> p (m t)").bitcast(I32),
+                in_=codes[:].bitcast(I32),
+            )
+
+        units = {
+            "xT": transpose_x, "xe": group_x, "xq": quantize_x, "ec": round_e, "eq": quantize_e, "mq": quantize_m,
+        }
+        halves = {"s1": stage1, "H": residual, "sc": weigh, "eT": transpose_e, "ee": keep_e, "s2": stage2, "M": mix,
+                  "s3": stage3, "ye": store_y, "yc": round_y, "yT": transpose_y, "yte": group_y, "yq": quantize_y}
+        for s in range(-3, 16):
+            for item in SCHED.split():
+                unit, lag = item.split(":")
+                if unit[0] == "w":
+                    for step, slot, what, n in W_PLAN:
+                        if step == s and slot == int(lag):
+                            if what == "q":
+                                quantize_w(n)
+                            else:
+                                group_w(n, what)
+                    continue
+                j = s - int(lag)
+                if (unit, j) in MOVED:
+                    continue
+                if unit == "mv":
+                    for key, where in MOVED.items():
+                        if where == (s, int(lag)):
+                            if key[0] in units:
+                                units[key[0]](key[1])
+                            else:
+                                halves[key[0][:-1]](key[1], int(key[0][-1]))
+                    continue
+                if 0 <= j < TILES:
+                    if unit in units:
+                        units[unit](j)
+                    else:
+                        halves[unit[:-1]](j, int(unit[-1]))
+                    if unit == "xT" and j == 1:
+                        widen_guide()
+                        make_weights()
+        for q in range(4):
+            queue = nc.sync if q % 2 == 0 else nc.scalar
+            queue.dma_start(
+                out=out_2.bitcast(I32)[:, 4 * q : 4 * q + 4, :].rearrange("g r m -> r g m"),
+                in_=y_plane[32 * q : 32 * q + 4, :, :].bitcast(I32),
+            )

@@ -21,18 +21,13 @@ TILES = T // P
 HALF = 512
 BANKS = 8
 
-SCALE_ENG = "SSSS"
-ECAST = "SSVSSS"
-YC = ["VV"] * 5 + ["PP"]
-YE = ["SS"] * 5 + ["SV"]
-YTE = ["SS"] * 5 + ["SV"]
-WSPLIT = 56
-MOVED = {("xq", 1): (-1, 1)}
-XEVAC = "SS"
-EB = 12
-SCHED = "mv:0 w:-1 yT0:9 yT1:9 s10:0 s11:0 H0:0 sc0:0 H1:0 sc1:0 eT0:1 eT1:1 ee0:1 ee1:1 xT:-2 xe:-2 s20:5 s21:5 yte0:9 yte1:9 s30:7 s31:7 xq:-1 w:0 ec:3 M0:5 M1:5 ye0:7 ye1:7 eq:4 yq0:9 yq1:9 w:1 mq:5 yc0:7 yc1:7 w:2 mv:1"
-W_PLAN = [[0,0,"v",0],[0,2,"s",0],[1,0,"q",0],[1,0,"v",2],[1,2,"s",2],[2,0,"q",2],[2,0,"v",1],[2,2,"s",1],[3,0,"q",1],[3,0,"v",3],[3,2,"s",3],[4,0,"q",3],[4,0,"v",4],[4,2,"s",4],[5,0,"q",4],[5,0,"v",5],[5,2,"s",5],[6,-1,"S",6],[6,0,"q",5],[6,0,"V",7],[6,1,"q",7],[6,2,"q",6]]
-LOADS = "x0 x1 w x2 a0 x3 a1 b0 x4 b1 x5"
+STAGE2_LAG = TILES - 1
+STAGE3_LAG = STAGE2_LAG + 2
+PLANES_LAG = STAGE3_LAG + 2
+
+PARTS = 4
+VECTOR_PIECES = 3
+SCALAR_PIECES = 2
 
 
 def tile_guided_hidden_noise_head_k1_kernel(tc, x, guide, w1_words, w1_scales, w2, w3, out_0, out_1, out_2):
@@ -46,28 +41,25 @@ def tile_guided_hidden_noise_head_k1_kernel(tc, x, guide, w1_words, w1_scales, w
         fills = []
 
         def next_bank():
-            fills.append(len(fills))
-            return psum.tile([P, HALF], F32, name="bank", tag="bank%d" % (fills[-1] % BANKS))
+            fills.append(len(fills) % BANKS)
+            return psum.tile([P, HALF], F32, name="bank", tag="bank%d" % fills[-1])
 
-        def copy_on(engine, out, in_):
-            if engine == "S":
-                nc.scalar.copy(out=out, in_=in_)
-            else:
-                nc.vector.tensor_copy(out=out, in_=in_)
+        def half(h):
+            return slice(h * HALF, (h + 1) * HALF)
 
-        w1_plane = keep.tile([P, 2, D], U8, name="w1_plane", align_bytes=64)
-        nc.vector.memset(w1_plane[:].bitcast(I32), 0)
+        def block(i):
+            return slice(i * P, (i + 1) * P)
+
         guide_rows = keep.tile([P, P], BF16, name="guide_rows")
         nc.vector.memset(guide_rows[:], 0.0)
-        warm = keep.tile([P, 2], F32, name="warm")
-        nc.vector.memset(warm[:], 0.0)
+        w1_plane = keep.tile([P, 2, D], U8, name="w1_plane", align_bytes=64)
+        nc.vector.memset(w1_plane[:].bitcast(I32), 0)
         ident = keep.tile([P, P], F32, name="ident")
         make_identity(nc, ident[:])
         nc.scalar.dma_start(out=guide_rows[0:TILES, :], in_=guide.rearrange("(j i) -> j i", i=P))
-        if "S" in SCALE_ENG:
-            nc.scalar.activation(out=warm[:, 1:2], in_=warm[:, 0:1], func=ACT.Copy, scale=1.0)
 
         x_rows = {}
+        w1_codes = {}
         w_raw = {}
 
         def load_x(j):
@@ -75,155 +67,152 @@ def tile_guided_hidden_noise_head_k1_kernel(tc, x, guide, w1_words, w1_scales, w
                 x_rows[j, b] = keep.tile([P, D], BF16, name="x_rows%d_%d" % (j, b))
                 nc.sync.dma_start(out=x_rows[j, b][:], in_=x[b * T + j * P : b * T + (j + 1) * P, :])
 
-        def load_w(n):
-            w = w2 if n < 4 else w3
-            g = n % 2
-            raw = keep.tile([P, 4, D], BF16, name="w_raw%d" % n)
-            nc.sync.dma_start(out=raw[:], in_=w[g * HALF : (g + 1) * HALF, :].rearrange("(p j) c -> p j c", j=4))
-            w_raw[n] = raw[:, :, 0:HALF]
-            w_raw[n + 2] = raw[:, :, HALF:D]
-
-        w1_codes = keep.tile([P, 2, 2 * D], U8, name="w1_codes", align_bytes=64)
-
         def load_w1():
             for q in range(4):
                 nc.sync.dma_start(
                     out=w1_plane[32 * q : 32 * q + 4, :, :].bitcast(I32),
                     in_=w1_scales.bitcast(I32)[:, 4 * q : 4 * q + 4, :].rearrange("g r n -> r g n"),
                 )
-            nc.sync.dma_start(out=w1_codes[:].bitcast(I32), in_=w1_words.bitcast(I32).rearrange("g p n -> p g n"))
-
-        for item in LOADS.split():
-            if item == "w":
-                load_w1()
-            elif item[0] == "x":
-                load_x(int(item[1]))
-            else:
-                load_w(int(item[1]) + (0 if item[0] == "a" else 4))
-
-        guide_f32 = keep.tile([P, P], F32, name="guide_f32")
-        weight = keep.tile([P, 2, 8], F32, name="weight")
-
-        def widen_guide():
-            nc.vector.tensor_copy(out=guide_f32[:], in_=guide_rows[:])
-
-        def make_weights():
-            bank = next_bank()
-            nc.tensor.transpose(bank[:, 0:P], guide_f32[:], ident[:])
-            nc.vector.tensor_copy(out=weight[:, 0, :], in_=bank[:, 0:8])
-            nc.vector.tensor_scalar(out=weight[:, 1, :], in0=bank[:, 0:8], scalar1=-1.0, scalar2=1.0, op0=ALU.mult, op1=ALU.add)
-
-        w_codes = {}
-        w_plane = {}
-        w_grouped = {}
-
-        def group_w(n, engine):
-            if n not in w_grouped:
-                w_grouped[n] = work.tile([P, 4 * HALF], BF16, name="w_grouped", bufs=3, align_bytes=64)
-            lo, hi = {"V": (0, 64), "S": (0, 64), "v": (0, WSPLIT), "s": (WSPLIT, 64)}[engine]
-            if n < 4:
-                copy_on(
-                    engine.replace("v", "V").replace("s", "S"),
-                    w_grouped[n][:].rearrange("p (t c m j) -> p c t m j", t=4, m=2, j=4)[:, lo:hi],
-                    w_raw[n].rearrange("p j (c m t) -> p c t m j", m=2, t=4)[:, lo:hi],
-                )
-            else:
-                copy_on(
-                    engine.replace("v", "V").replace("s", "S"),
-                    w_grouped[n][:].rearrange("p (c i j) -> p c j i", i=4, j=4)[:, 2 * lo : 2 * hi],
-                    w_raw[n].rearrange("p j (c i) -> p c j i", i=4)[:, 2 * lo : 2 * hi],
+            for h in range(2):
+                w1_codes[h] = keep.tile([P, 2, 2 * HALF], U8, name="w1_codes%d" % h, align_bytes=64)
+                nc.sync.dma_start(
+                    out=w1_codes[h][:].bitcast(I32),
+                    in_=w1_words.bitcast(I32)[:, :, h * 256 : (h + 1) * 256].rearrange("g p n -> p g n"),
                 )
 
-        def quantize_w(n):
-            w_codes[n] = keep.tile([P, HALF], U32, name="w_codes%d" % n, align_bytes=64)
-            w_plane[n] = keep.tile([P, HALF], U8, name="w_plane%d" % n, align_bytes=64)
-            nc.vector.quantize_mx(out=w_codes[n][:].bitcast(FP8X4), scales=w_plane[n][:], in_=w_grouped[n][:])
+        def load_w(stage, g):
+            w_raw[stage, g] = keep.tile([P, 4, D], BF16, name="w_raw%d_%d" % (stage, g))
+            source = {2: w2, 3: w3}[stage]
+            nc.sync.dma_start(out=w_raw[stage, g][:], in_=source[half(g), :].rearrange("(p j) c -> p j c", j=4))
 
+        load_x(0)
+        load_x(1)
+        load_w1()
+        load_w(2, 0)
+        load_x(2)
+        load_x(3)
+        load_w(2, 1)
+        load_w(3, 0)
+        load_x(4)
+        load_w(3, 1)
+        load_x(5)
+
+        guide_wide = keep.tile([P, P], F32, name="guide_wide")
+        weight = keep.tile([P, 2, TILES], F32, name="weight")
         tiles = {}
 
-        def quantize(kind, j, width):
-            codes = work.tile([P, width // 4], U32, name=kind + "_codes", bufs=4, align_bytes=64)
-            plane = work.tile([P, width // 4], U8, name=kind + "_plane", bufs=4, align_bytes=64)
-            nc.vector.quantize_mx(out=codes[:].bitcast(FP8X4), scales=plane[:], in_=tiles[kind + "_grouped", j][:])
+        def turn_guide():
+            nc.vector.tensor_copy(out=guide_wide[:], in_=guide_rows[:])
+            tiles["guide_bank"] = next_bank()
+            nc.tensor.transpose(tiles["guide_bank"][:, 0:P], guide_wide[:], ident[:])
+
+        def make_weights():
+            turned = tiles["guide_bank"][:, 0:TILES]
+            nc.scalar.activation(out=weight[:, 0, :], in_=turned, func=ACT.Copy)
+            nc.scalar.activation(out=weight[:, 1, :], in_=turned, func=ACT.Copy, scale=-1.0, bias=1.0)
+
+        chunks = [(stage, g, h) for stage in (2, 3) for g in range(2) for h in range(2)]
+        pieces = [(chunk, part) for chunk in chunks for part in range(PARTS)]
+        w_grouped = {}
+        w_codes = {}
+        w_plane = {}
+
+        def group_pieces(count, copy):
+            for chunk, part in pieces[:count]:
+                stage, g, h = chunk
+                if part == 0:
+                    w_grouped[chunk] = work.tile([P, 4 * HALF], BF16, name="w_grouped", bufs=4, align_bytes=64)
+                raw = w_raw[stage, g][:, :, half(h)]
+                if stage == 2:
+                    share = slice(16 * part, 16 * part + 16)
+                    copy(
+                        out=w_grouped[chunk][:].rearrange("p (t c e j) -> p c t e j", t=4, e=2, j=4)[:, share],
+                        in_=raw.rearrange("p j (c e t) -> p c t e j", e=2, t=4)[:, share],
+                    )
+                else:
+                    share = slice(32 * part, 32 * part + 32)
+                    copy(
+                        out=w_grouped[chunk][:].rearrange("p (c i j) -> p c j i", i=4, j=4)[:, share],
+                        in_=raw.rearrange("p j (c i) -> p c j i", i=4)[:, share],
+                    )
+                pieces.remove((chunk, part))
+
+        def quantize_finished_chunks():
+            for chunk in chunks:
+                if chunk not in w_codes and (chunk, PARTS - 1) not in pieces:
+                    w_codes[chunk] = keep.tile([P, HALF], U32, name="w_codes%d_%d_%d" % chunk, align_bytes=64)
+                    w_plane[chunk] = keep.tile([P, HALF], U8, name="w_plane%d_%d_%d" % chunk, align_bytes=64)
+                    nc.vector.quantize_mx(
+                        out=w_codes[chunk][:].bitcast(FP8X4), scales=w_plane[chunk][:], in_=w_grouped[chunk][:]
+                    )
+
+        def quantize(kind, j):
+            grouped = tiles[kind + "_grouped", j]
+            words = grouped.shape[1] // 4
+            codes = work.tile([P, words], U32, name=kind + "_codes", bufs=3, align_bytes=64)
+            plane = work.tile([P, words], U8, name=kind + "_plane", bufs=3, align_bytes=64)
+            nc.vector.quantize_mx(out=codes[:].bitcast(FP8X4), scales=plane[:], in_=grouped[:])
             tiles[kind + "_codes", j] = codes
             tiles[kind + "_plane", j] = plane
 
-        def transpose_x(j):
+        def turn_x(j):
             for b in range(2):
                 words = x_rows[j, b][:].bitcast(F32)
-                bank = next_bank()
-                tiles["x_bank", j, b] = bank
+                tiles["x_bank", j, b] = next_bank()
                 for g in range(2):
                     for u in range(2):
                         nc.tensor.transpose(
-                            bank[:, (2 * g + u) * P : (2 * g + u + 1) * P], words[:, 256 * g + u : 256 * (g + 1) : 2], ident[:]
+                            tiles["x_bank", j, b][:, block(2 * g + u)], words[:, 256 * g + u : 256 * (g + 1) : 2], ident[:]
                         )
 
         def group_x(j):
-            grouped = work.tile([P, 2 * D], BF16, name="x_grouped", bufs=3, align_bytes=64)
-            tiles["x_grouped", j] = grouped
+            tiles["x_grouped", j] = work.tile([P, 2 * D], BF16, name="x_grouped", bufs=3, align_bytes=64)
             for b in range(2):
-                copy_on(
-                    XEVAC[b],
-                    grouped[:, b * D : (b + 1) * D].bitcast(F32).rearrange("p (g r u) -> p g r u", g=2, u=2),
-                    tiles["x_bank", j, b][:].rearrange("p (g u r) -> p g r u", g=2, u=2),
+                nc.scalar.copy(
+                    out=tiles["x_grouped", j][:, b * D : (b + 1) * D].bitcast(F32).rearrange("p (g r u) -> p g r u", g=2, u=2),
+                    in_=tiles["x_bank", j, b][:].rearrange("p (g u r) -> p g r u", g=2, u=2),
                 )
 
-        def quantize_x(j):
-            quantize("x", j, 2 * D)
-
         def stage1(j, h):
-            codes, plane = tiles["x_codes", j], tiles["x_plane", j]
             for b in range(2):
-                bank = next_bank()
-                tiles["h_bank", j, h, b] = bank
+                tiles["h_bank", j, h, b] = next_bank()
                 for g in range(2):
-                    cols = slice((2 * b + g) * P, (2 * b + g + 1) * P)
                     nc.tensor.matmul_mx(
-                        out=bank[:],
-                        lhsT=codes[:, cols].bitcast(FP8X4),
-                        lhsT_scale=plane[:, cols],
-                        rhs=w1_codes[:, g, 2 * h * HALF : 2 * (h + 1) * HALF].bitcast(FP4X4),
-                        rhs_scale=w1_plane[:, g, h * HALF : (h + 1) * HALF],
+                        out=tiles["h_bank", j, h, b][:],
+                        lhsT=tiles["x_codes", j][:, block(2 * b + g)].bitcast(FP8X4),
+                        lhsT_scale=tiles["x_plane", j][:, block(2 * b + g)],
+                        rhs=w1_codes[h][:, g, :].bitcast(FP4X4),
+                        rhs_scale=w1_plane[:, g, half(h)],
                         start=(g == 0),
                         stop=(g == 1),
                     )
 
-        def residual(j, h):
+        def residual_and_weigh(j, h):
             for b in range(2):
-                hidden = work.tile([P, HALF], F32, name="hidden", bufs=6)
-                tiles["hidden", j, h, b] = hidden
+                tiles["term", j, h, b] = work.tile([P, HALF], F32, name="term", bufs=8)
                 nc.vector.scalar_tensor_tensor(
-                    out=hidden[:].rearrange("p (t m) -> p t m", t=4),
+                    out=tiles["term", j, h, b][:].rearrange("p (t m) -> p t m", t=4),
                     in0=tiles["h_bank", j, h, b][:].rearrange("p (m t) -> p t m", t=4),
                     scalar=0.0,
-                    in1=x_rows[j, b][:, h * HALF : (h + 1) * HALF].rearrange("p (m t) -> p t m", t=4),
+                    in1=x_rows[j, b][:, half(h)].rearrange("p (m t) -> p t m", t=4),
                     op0=ALU.max,
                     op1=ALU.add,
                 )
-
-        def weigh(j, h):
             for b in range(2):
-                term = work.tile([P, HALF], F32, name="term", bufs=8)
-                tiles["term", j, h, b] = term
-                hidden = tiles["hidden", j, h, b]
+                term = tiles["term", j, h, b]
                 factor = weight[:, b, j : j + 1]
-                engine = SCALE_ENG[2 * h + b]
-                if engine == "S":
-                    nc.scalar.activation(out=term[:], in_=hidden[:], func=ACT.Copy, scale=factor)
-                elif engine == "G":
-                    nc.gpsimd.tensor_scalar(out=term[:], in0=hidden[:], scalar1=factor, scalar2=0.0, op0=ALU.mult, op1=ALU.add)
+                if h == 0:
+                    nc.gpsimd.tensor_scalar(out=term[:], in0=term[:], scalar1=factor, scalar2=0.0, op0=ALU.mult, op1=ALU.add)
                 else:
-                    nc.vector.tensor_scalar(out=term[:], in0=hidden[:], scalar1=factor, scalar2=None, op0=ALU.mult)
+                    nc.scalar.activation(out=term[:], in_=term[:], func=ACT.Copy, scale=factor)
 
-        def transpose_e(j, h):
-            bank = next_bank()
-            tiles["e_bank", j, h] = bank
+        def turn_e(j, h):
+            tiles["e_bank", j, h] = next_bank()
             for t in range(4):
                 for b in range(2):
                     nc.tensor.matmul(
-                        bank[:, t * P : (t + 1) * P],
-                        lhsT=tiles["term", j, h, b][:, t * P : (t + 1) * P],
+                        tiles["e_bank", j, h][:, block(t)],
+                        lhsT=tiles["term", j, h, b][:, block(t)],
                         rhs=ident[:],
                         start=(b == 0),
                         stop=(b == 1),
@@ -231,155 +220,169 @@ def tile_guided_hidden_noise_head_k1_kernel(tc, x, guide, w1_words, w1_scales, w
                     )
 
         def keep_e(j, h):
-            bank = tiles["e_bank", j, h]
-            exact = work.tile([P, HALF], F32, name="e_exact", bufs=EB)
-            tiles["e_exact", j, h] = exact
-            nc.scalar.copy(out=exact[:].rearrange("p (n t) -> p n t", t=4), in_=bank[:].rearrange("p (t n) -> p n t", t=4))
+            tiles["e_exact", j, h] = work.tile([P, HALF], F32, name="e_exact", bufs=2 * TILES)
+            nc.scalar.copy(
+                out=tiles["e_exact", j, h][:].rearrange("p (n t) -> p n t", t=4),
+                in_=tiles["e_bank", j, h][:].rearrange("p (t n) -> p n t", t=4),
+            )
 
         def round_e(j):
-            tiles["e_grouped", j] = work.tile([P, D], BF16, name="e_grouped", bufs=3, align_bytes=64)
+            tiles["e_grouped", j] = work.tile([P, D], BF16, name="e_grouped", bufs=1, align_bytes=64)
             for h in range(2):
-                dst = tiles["e_grouped", j][:, h * HALF : (h + 1) * HALF]
-                if ECAST[j] == "V":
-                    nc.vector.tensor_copy(out=dst, in_=tiles["e_exact", j, h][:])
+                rounded = tiles["e_grouped", j][:, half(h)]
+                exact = tiles["e_exact", j, h]
+                if h == 0 and j >= 2:
+                    nc.gpsimd.tensor_scalar(out=rounded, in0=exact[:], scalar1=1.0, scalar2=0.0, op0=ALU.mult, op1=ALU.add)
                 else:
-                    nc.scalar.copy(out=dst, in_=tiles["e_exact", j, h][:])
-
-        def quantize_e(j):
-            quantize("e", j, D)
+                    nc.scalar.copy(out=rounded, in_=exact[:])
 
         def stage2(j, h):
-            codes, plane = tiles["e_codes", j], tiles["e_plane", j]
-            bank = next_bank()
-            tiles["m_bank", j, h] = bank
+            tiles["m_bank", j, h] = next_bank()
             for t in range(4):
                 for g in range(2):
                     nc.tensor.matmul_mx(
-                        out=bank[:, t * P : (t + 1) * P],
-                        lhsT=w_codes[2 * h + g][:, t * P : (t + 1) * P].bitcast(FP8X4),
-                        lhsT_scale=w_plane[2 * h + g][:, t * P : (t + 1) * P],
-                        rhs=codes[:, g * P : (g + 1) * P].bitcast(FP8X4),
-                        rhs_scale=plane[:, g * P : (g + 1) * P],
+                        out=tiles["m_bank", j, h][:, block(t)],
+                        lhsT=w_codes[2, g, h][:, block(t)].bitcast(FP8X4),
+                        lhsT_scale=w_plane[2, g, h][:, block(t)],
+                        rhs=tiles["e_codes", j][:, block(g)].bitcast(FP8X4),
+                        rhs_scale=tiles["e_plane", j][:, block(g)],
                         start=(g == 0),
                         stop=(g == 1),
                     )
 
-        def mix(j, h):
-            if h == 0:
-                tiles["m_grouped", j] = work.tile([P, D], BF16, name="m_grouped", bufs=3, align_bytes=64)
-            nc.vector.tensor_tensor(
-                out=tiles["m_grouped", j][:, h * HALF : (h + 1) * HALF].rearrange("p (n t) -> p n t", t=4),
-                in0=tiles["m_bank", j, h][:].rearrange("p (t n) -> p n t", t=4),
-                in1=tiles["e_exact", j, h][:].rearrange("p (n t) -> p n t", t=4),
-                op=ALU.add,
-            )
-
-        def quantize_m(j):
-            quantize("m", j, D)
+        def mix(j):
+            tiles["m_grouped", j] = work.tile([P, D], BF16, name="m_grouped", bufs=3, align_bytes=64)
+            for h in range(2):
+                nc.vector.tensor_tensor(
+                    out=tiles["m_grouped", j][:, half(h)].rearrange("p (n t) -> p n t", t=4),
+                    in0=tiles["m_bank", j, h][:].rearrange("p (t n) -> p n t", t=4),
+                    in1=tiles["e_exact", j, h][:].rearrange("p (n t) -> p n t", t=4),
+                    op=ALU.add,
+                )
 
         def stage3(j, h):
-            codes, plane = tiles["m_codes", j], tiles["m_plane", j]
-            bank = next_bank()
-            tiles["y_bank", j, h] = bank
+            tiles["y_bank", j, h] = next_bank()
             for g in range(2):
                 nc.tensor.matmul_mx(
-                    out=bank[:],
-                    lhsT=codes[:, g * P : (g + 1) * P].bitcast(FP8X4),
-                    lhsT_scale=plane[:, g * P : (g + 1) * P],
-                    rhs=w_codes[4 + 2 * h + g][:].bitcast(FP8X4),
-                    rhs_scale=w_plane[4 + 2 * h + g][:],
+                    out=tiles["y_bank", j, h][:],
+                    lhsT=tiles["m_codes", j][:, block(g)].bitcast(FP8X4),
+                    lhsT_scale=tiles["m_plane", j][:, block(g)],
+                    rhs=w_codes[3, g, h][:].bitcast(FP8X4),
+                    rhs_scale=w_plane[3, g, h][:],
                     start=(g == 0),
                     stop=(g == 1),
                 )
 
-        def store_y(j, h):
-            bank = tiles["y_bank", j, h]
-            result = work.tile([P, HALF], F32, name="result", bufs=6)
-            rounded = work.tile([P, HALF], BF16, name="y_rounded", bufs=6)
-            tiles["result", j, h] = result
-            tiles["y_rounded", j, h] = rounded
-            if YC[j][h] == "P":
-                copy_on(
-                    YE[j][h],
-                    rounded[:].rearrange("p (u m e) -> p u m e", u=2, e=2),
-                    bank[:].rearrange("p (m u e) -> p u m e", u=2, e=2),
-                )
-            copy_on(YE[j][h], result[:], bank[:])
-            nc.sync.dma_start(out=out_0[j * P : (j + 1) * P, h * HALF : (h + 1) * HALF], in_=result[:])
+        def round_y(j, h, source, copy):
+            tiles["y_rounded", j, h] = work.tile([P, HALF], BF16, name="y_rounded", bufs=6)
+            copy(
+                out=tiles["y_rounded", j, h][:].rearrange("p (u m e) -> p u m e", u=2, e=2),
+                in_=source.rearrange("p (m u e) -> p u m e", u=2, e=2),
+            )
 
-        def round_y(j, h):
-            if YC[j][h] != "P":
-                copy_on(
-                    YC[j][h],
-                    tiles["y_rounded", j, h][:].rearrange("p (u m e) -> p u m e", u=2, e=2),
-                    tiles["result", j, h][:].rearrange("p (m u e) -> p u m e", u=2, e=2),
-                )
+        def store_y(j):
+            tiles["y", j] = work.tile([P, D], F32, name="y", bufs=4)
+            for h in range(2):
+                nc.scalar.copy(out=tiles["y", j][:, half(h)], in_=tiles["y_bank", j, h][:])
+            nc.sync.dma_start(out=out_0[block(j), :], in_=tiles["y", j][:])
 
-        def transpose_y(j, h):
+        def finish_last_y():
+            j = TILES - 1
+            tiles["y", j] = work.tile([P, D], F32, name="y", bufs=4)
+            for h in range(2):
+                round_y(j, h, tiles["y_bank", j, h][:], both_copies[h])
+            for h in range(2):
+                both_copies[h](out=tiles["y", j][:, half(h)], in_=tiles["y_bank", j, h][:])
+                nc.sync.dma_start(out=out_0[block(j), half(h)], in_=tiles["y", j][:, half(h)])
+
+        def turn_y(j, h):
             words = tiles["y_rounded", j, h][:].bitcast(F32)
-            bank = next_bank()
-            tiles["t_bank", j, h] = bank
+            tiles["t_bank", j, h] = next_bank()
             for u in range(2):
-                nc.tensor.transpose(bank[:, u * P : (u + 1) * P], words[:, u * P : (u + 1) * P], ident[:])
+                nc.tensor.transpose(tiles["t_bank", j, h][:, block(u)], words[:, block(u)], ident[:])
 
-        def group_y(j, h):
-            grouped = work.tile([P, HALF], BF16, name="y_grouped", bufs=4, align_bytes=64)
-            tiles["y_grouped", j, h] = grouped
-            copy_on(
-                YTE[j][h],
-                grouped[:].bitcast(F32).rearrange("p (r u) -> p r u", u=2),
-                tiles["t_bank", j, h][:, 0 : 2 * P].rearrange("p (u r) -> p r u", u=2),
+        def group_y(j, h, copy):
+            tiles["y_grouped", j, h] = work.tile([P, HALF], BF16, name="y_grouped", bufs=4, align_bytes=64)
+            copy(
+                out=tiles["y_grouped", j, h][:].bitcast(F32).rearrange("p (r u) -> p r u", u=2),
+                in_=tiles["t_bank", j, h][:, 0 : 2 * P].rearrange("p (u r) -> p r u", u=2),
             )
 
         y_plane = keep.tile([P, 2, T], U8, name="y_plane", align_bytes=64)
 
-        def quantize_y(j, h):
-            codes = work.tile([P, P], U32, name="y_codes", bufs=6, align_bytes=64)
-            nc.vector.quantize_mx(
-                out=codes[:].bitcast(FP8X4),
-                scales=y_plane[:, h, j * P : (j + 1) * P],
-                in_=tiles["y_grouped", j, h][:],
-            )
+        def quantize_y(j):
+            codes = work.tile([P, 2, P], U32, name="y_codes", bufs=4, align_bytes=64)
+            for g in range(2):
+                nc.vector.quantize_mx(
+                    out=codes[:, g, :].bitcast(FP8X4), scales=y_plane[:, g, block(j)], in_=tiles["y_grouped", j, g][:]
+                )
             nc.sync.dma_start(
-                out=out_1[h, :, j * P : (j + 1) * P, :].rearrange("p m t -> p (m t)").bitcast(I32),
-                in_=codes[:].bitcast(I32),
+                out=out_1[:, :, block(j), :].rearrange("g p m t -> p g (m t)").bitcast(I32), in_=codes[:].bitcast(I32)
             )
 
-        units = {
-            "xT": transpose_x, "xe": group_x, "xq": quantize_x, "ec": round_e, "eq": quantize_e, "mq": quantize_m,
-        }
-        halves = {"s1": stage1, "H": residual, "sc": weigh, "eT": transpose_e, "ee": keep_e, "s2": stage2, "M": mix,
-                  "s3": stage3, "ye": store_y, "yc": round_y, "yT": transpose_y, "yte": group_y, "yq": quantize_y}
-        for s in range(-3, 16):
-            for item in SCHED.split():
-                unit, lag = item.split(":")
-                if unit[0] == "w":
-                    for step, slot, what, n in W_PLAN:
-                        if step == s and slot == int(lag):
-                            if what == "q":
-                                quantize_w(n)
-                            else:
-                                group_w(n, what)
-                    continue
-                j = s - int(lag)
-                if (unit, j) in MOVED:
-                    continue
-                if unit == "mv":
-                    for key, where in MOVED.items():
-                        if where == (s, int(lag)):
-                            if key[0] in units:
-                                units[key[0]](key[1])
-                            else:
-                                halves[key[0][:-1]](key[1], int(key[0][-1]))
-                    continue
-                if 0 <= j < TILES:
-                    if unit in units:
-                        units[unit](j)
-                    else:
-                        halves[unit[:-1]](j, int(unit[-1]))
-                    if unit == "xT" and j == 1:
-                        widen_guide()
-                        make_weights()
+        both_copies = (nc.scalar.copy, nc.vector.tensor_copy)
+
+        turn_x(0)
+        group_x(0)
+        turn_x(1)
+        turn_guide()
+        group_x(1)
+        make_weights()
+        quantize("x", 0)
+        group_pieces(SCALAR_PIECES, nc.scalar.copy)
+        quantize("x", 1)
+
+        for step in range(TILES + PLANES_LAG):
+            j1, j2, j3, jp = step, step - STAGE2_LAG, step - STAGE3_LAG, step - PLANES_LAG
+            extra = 1 if step == 0 else 0
+            if jp >= 0:
+                turn_y(jp, 0)
+                turn_y(jp, 1)
+            if j1 < TILES:
+                stage1(j1, 0)
+                stage1(j1, 1)
+                residual_and_weigh(j1, 0)
+                residual_and_weigh(j1, 1)
+            if 1 <= j1 <= TILES:
+                turn_e(j1 - 1, 0)
+                turn_e(j1 - 1, 1)
+                keep_e(j1 - 1, 0)
+                keep_e(j1 - 1, 1)
+            if j1 + 2 < TILES:
+                turn_x(j1 + 2)
+                group_x(j1 + 2)
+            if 0 <= j2 < TILES:
+                stage2(j2, 0)
+                stage2(j2, 1)
+            if jp >= 0:
+                group_y(jp, 0, nc.scalar.copy)
+                group_y(jp, 1, both_copies[jp == TILES - 1])
+            if 0 <= j3 < TILES:
+                stage3(j3, 0)
+                stage3(j3, 1)
+            if 2 <= j1 + 1 < TILES:
+                quantize("x", j1 + 1)
+            if 0 <= j2 + 1 < TILES:
+                quantize("e", j2 + 1)
+            if 0 <= j2 < TILES:
+                mix(j2)
+            quantize_finished_chunks()
+            group_pieces(VECTOR_PIECES + extra, nc.vector.tensor_copy)
+            if 0 <= j2 + 2 < TILES:
+                round_e(j2 + 2)
+            if jp >= 0:
+                quantize_y(jp)
+            if 0 <= j3 < TILES - 1:
+                store_y(j3)
+            if j3 == TILES - 1:
+                finish_last_y()
+            group_pieces(SCALAR_PIECES + extra, nc.scalar.copy)
+            if 0 <= j2 < TILES:
+                quantize("m", j2)
+            if 0 <= j3 < TILES - 1:
+                round_y(j3, 0, tiles["y", j3][:, half(0)], nc.vector.tensor_copy)
+                round_y(j3, 1, tiles["y", j3][:, half(1)], nc.vector.tensor_copy)
+
         for q in range(4):
             queue = nc.sync if q % 2 == 0 else nc.scalar
             queue.dma_start(

from contextlib import ExitStack

import concourse.mybir as mybir
from concourse.masks import make_identity

T, D = 768, 1024
FLOPS = 2 * (2 * T + T + T) * D * D

F32 = mybir.dt.float32
BF16 = mybir.dt.bfloat16
I32 = mybir.dt.int32
U32 = mybir.dt.uint32
U8 = mybir.dt.uint8
FP8X4 = mybir.dt.float8_e4m3fn_x4
FP4X4 = mybir.dt.float4_e2m1fn_x4
ALU = mybir.AluOpType
ACT = mybir.ActivationFunctionType

P = 128
TILES = T // P
HALF = 512
BANKS = 8

STAGE2_LAG = TILES - 1
STAGE3_LAG = STAGE2_LAG + 2
PLANES_LAG = STAGE3_LAG + 2

PARTS = 4
VECTOR_PIECES = 3
SCALAR_PIECES = 2


def tile_guided_hidden_noise_head_k1_kernel(tc, x, guide, w1_words, w1_scales, w2, w3, out_0, out_1, out_2):
    nc = tc.nc
    with ExitStack() as ctx:
        keep = ctx.enter_context(tc.tile_pool(name="keep", bufs=1))
        work = ctx.enter_context(tc.tile_pool(name="work", bufs=2))
        psum = ctx.enter_context(tc.psum_pool(name="psum", bufs=1))
        ctx.enter_context(tc.manual_schedule())

        fills = []

        def next_bank():
            fills.append(len(fills) % BANKS)
            return psum.tile([P, HALF], F32, name="bank", tag="bank%d" % fills[-1])

        def half(h):
            return slice(h * HALF, (h + 1) * HALF)

        def block(i):
            return slice(i * P, (i + 1) * P)

        guide_rows = keep.tile([P, P], BF16, name="guide_rows")
        nc.vector.memset(guide_rows[:], 0.0)
        w1_plane = keep.tile([P, 2, D], U8, name="w1_plane", align_bytes=64)
        nc.vector.memset(w1_plane[:].bitcast(I32), 0)
        ident = keep.tile([P, P], F32, name="ident")
        make_identity(nc, ident[:])
        nc.scalar.dma_start(out=guide_rows[0:TILES, :], in_=guide.rearrange("(j i) -> j i", i=P))

        x_rows = {}
        w1_codes = {}
        w_raw = {}

        def load_x(j):
            for b in range(2):
                x_rows[j, b] = keep.tile([P, D], BF16, name="x_rows%d_%d" % (j, b))
                nc.sync.dma_start(out=x_rows[j, b][:], in_=x[b * T + j * P : b * T + (j + 1) * P, :])

        def load_w1():
            for q in range(4):
                nc.sync.dma_start(
                    out=w1_plane[32 * q : 32 * q + 4, :, :].bitcast(I32),
                    in_=w1_scales.bitcast(I32)[:, 4 * q : 4 * q + 4, :].rearrange("g r n -> r g n"),
                )
            for h in range(2):
                w1_codes[h] = keep.tile([P, 2, 2 * HALF], U8, name="w1_codes%d" % h, align_bytes=64)
                nc.sync.dma_start(
                    out=w1_codes[h][:].bitcast(I32),
                    in_=w1_words.bitcast(I32)[:, :, h * 256 : (h + 1) * 256].rearrange("g p n -> p g n"),
                )

        def load_w(stage, g):
            w_raw[stage, g] = keep.tile([P, 4, D], BF16, name="w_raw%d_%d" % (stage, g))
            source = {2: w2, 3: w3}[stage]
            nc.sync.dma_start(out=w_raw[stage, g][:], in_=source[half(g), :].rearrange("(p j) c -> p j c", j=4))

        load_x(0)
        load_x(1)
        load_w1()
        load_w(2, 0)
        load_x(2)
        load_x(3)
        load_w(2, 1)
        load_w(3, 0)
        load_x(4)
        load_w(3, 1)
        load_x(5)

        guide_wide = keep.tile([P, P], F32, name="guide_wide")
        weight = keep.tile([P, 2, TILES], F32, name="weight")
        tiles = {}

        def turn_guide():
            nc.vector.tensor_copy(out=guide_wide[:], in_=guide_rows[:])
            tiles["guide_bank"] = next_bank()
            nc.tensor.transpose(tiles["guide_bank"][:, 0:P], guide_wide[:], ident[:])

        def make_weights():
            turned = tiles["guide_bank"][:, 0:TILES]
            nc.scalar.activation(out=weight[:, 0, :], in_=turned, func=ACT.Copy)
            nc.scalar.activation(out=weight[:, 1, :], in_=turned, func=ACT.Copy, scale=-1.0, bias=1.0)

        chunks = [(stage, g, h) for stage in (2, 3) for g in range(2) for h in range(2)]
        pieces = [(chunk, part) for chunk in chunks for part in range(PARTS)]
        w_grouped = {}
        w_codes = {}
        w_plane = {}

        def group_pieces(count, copy):
            for chunk, part in pieces[:count]:
                stage, g, h = chunk
                if part == 0:
                    w_grouped[chunk] = work.tile([P, 4 * HALF], BF16, name="w_grouped", bufs=4, align_bytes=64)
                raw = w_raw[stage, g][:, :, half(h)]
                if stage == 2:
                    share = slice(16 * part, 16 * part + 16)
                    copy(
                        out=w_grouped[chunk][:].rearrange("p (t c e j) -> p c t e j", t=4, e=2, j=4)[:, share],
                        in_=raw.rearrange("p j (c e t) -> p c t e j", e=2, t=4)[:, share],
                    )
                else:
                    share = slice(32 * part, 32 * part + 32)
                    copy(
                        out=w_grouped[chunk][:].rearrange("p (c i j) -> p c j i", i=4, j=4)[:, share],
                        in_=raw.rearrange("p j (c i) -> p c j i", i=4)[:, share],
                    )
                pieces.remove((chunk, part))

        def quantize_finished_chunks():
            for chunk in chunks:
                if chunk not in w_codes and (chunk, PARTS - 1) not in pieces:
                    w_codes[chunk] = keep.tile([P, HALF], U32, name="w_codes%d_%d_%d" % chunk, align_bytes=64)
                    w_plane[chunk] = keep.tile([P, HALF], U8, name="w_plane%d_%d_%d" % chunk, align_bytes=64)
                    nc.vector.quantize_mx(
                        out=w_codes[chunk][:].bitcast(FP8X4), scales=w_plane[chunk][:], in_=w_grouped[chunk][:]
                    )

        def quantize(kind, j):
            grouped = tiles[kind + "_grouped", j]
            words = grouped.shape[1] // 4
            codes = work.tile([P, words], U32, name=kind + "_codes", bufs=3, align_bytes=64)
            plane = work.tile([P, words], U8, name=kind + "_plane", bufs=3, align_bytes=64)
            nc.vector.quantize_mx(out=codes[:].bitcast(FP8X4), scales=plane[:], in_=grouped[:])
            tiles[kind + "_codes", j] = codes
            tiles[kind + "_plane", j] = plane

        def turn_x(j):
            for b in range(2):
                words = x_rows[j, b][:].bitcast(F32)
                tiles["x_bank", j, b] = next_bank()
                for g in range(2):
                    for u in range(2):
                        nc.tensor.transpose(
                            tiles["x_bank", j, b][:, block(2 * g + u)], words[:, 256 * g + u : 256 * (g + 1) : 2], ident[:]
                        )

        def group_x(j):
            tiles["x_grouped", j] = work.tile([P, 2 * D], BF16, name="x_grouped", bufs=3, align_bytes=64)
            for b in range(2):
                nc.scalar.copy(
                    out=tiles["x_grouped", j][:, b * D : (b + 1) * D].bitcast(F32).rearrange("p (g r u) -> p g r u", g=2, u=2),
                    in_=tiles["x_bank", j, b][:].rearrange("p (g u r) -> p g r u", g=2, u=2),
                )

        def stage1(j, h):
            for b in range(2):
                tiles["h_bank", j, h, b] = next_bank()
                for g in range(2):
                    nc.tensor.matmul_mx(
                        out=tiles["h_bank", j, h, b][:],
                        lhsT=tiles["x_codes", j][:, block(2 * b + g)].bitcast(FP8X4),
                        lhsT_scale=tiles["x_plane", j][:, block(2 * b + g)],
                        rhs=w1_codes[h][:, g, :].bitcast(FP4X4),
                        rhs_scale=w1_plane[:, g, half(h)],
                        start=(g == 0),
                        stop=(g == 1),
                    )

        def residual_and_weigh(j, h):
            for b in range(2):
                tiles["term", j, h, b] = work.tile([P, HALF], F32, name="term", bufs=8)
                nc.vector.scalar_tensor_tensor(
                    out=tiles["term", j, h, b][:].rearrange("p (t m) -> p t m", t=4),
                    in0=tiles["h_bank", j, h, b][:].rearrange("p (m t) -> p t m", t=4),
                    scalar=0.0,
                    in1=x_rows[j, b][:, half(h)].rearrange("p (m t) -> p t m", t=4),
                    op0=ALU.max,
                    op1=ALU.add,
                )
            for b in range(2):
                term = tiles["term", j, h, b]
                factor = weight[:, b, j : j + 1]
                if h == 0:
                    nc.gpsimd.tensor_scalar(out=term[:], in0=term[:], scalar1=factor, scalar2=0.0, op0=ALU.mult, op1=ALU.add)
                else:
                    nc.scalar.activation(out=term[:], in_=term[:], func=ACT.Copy, scale=factor)

        def turn_e(j, h):
            tiles["e_bank", j, h] = next_bank()
            for t in range(4):
                for b in range(2):
                    nc.tensor.matmul(
                        tiles["e_bank", j, h][:, block(t)],
                        lhsT=tiles["term", j, h, b][:, block(t)],
                        rhs=ident[:],
                        start=(b == 0),
                        stop=(b == 1),
                        is_transpose=True,
                    )

        def keep_e(j, h):
            tiles["e_exact", j, h] = work.tile([P, HALF], F32, name="e_exact", bufs=2 * TILES)
            nc.scalar.copy(
                out=tiles["e_exact", j, h][:].rearrange("p (n t) -> p n t", t=4),
                in_=tiles["e_bank", j, h][:].rearrange("p (t n) -> p n t", t=4),
            )

        def round_e(j):
            tiles["e_grouped", j] = work.tile([P, D], BF16, name="e_grouped", bufs=1, align_bytes=64)
            for h in range(2):
                rounded = tiles["e_grouped", j][:, half(h)]
                exact = tiles["e_exact", j, h]
                if h == 0 and j >= 2:
                    nc.gpsimd.tensor_scalar(out=rounded, in0=exact[:], scalar1=1.0, scalar2=0.0, op0=ALU.mult, op1=ALU.add)
                else:
                    nc.scalar.copy(out=rounded, in_=exact[:])

        def stage2(j, h):
            tiles["m_bank", j, h] = next_bank()
            for t in range(4):
                for g in range(2):
                    nc.tensor.matmul_mx(
                        out=tiles["m_bank", j, h][:, block(t)],
                        lhsT=w_codes[2, g, h][:, block(t)].bitcast(FP8X4),
                        lhsT_scale=w_plane[2, g, h][:, block(t)],
                        rhs=tiles["e_codes", j][:, block(g)].bitcast(FP8X4),
                        rhs_scale=tiles["e_plane", j][:, block(g)],
                        start=(g == 0),
                        stop=(g == 1),
                    )

        def mix(j):
            tiles["m_grouped", j] = work.tile([P, D], BF16, name="m_grouped", bufs=3, align_bytes=64)
            for h in range(2):
                nc.vector.tensor_tensor(
                    out=tiles["m_grouped", j][:, half(h)].rearrange("p (n t) -> p n t", t=4),
                    in0=tiles["m_bank", j, h][:].rearrange("p (t n) -> p n t", t=4),
                    in1=tiles["e_exact", j, h][:].rearrange("p (n t) -> p n t", t=4),
                    op=ALU.add,
                )

        def stage3(j, h):
            tiles["y_bank", j, h] = next_bank()
            for g in range(2):
                nc.tensor.matmul_mx(
                    out=tiles["y_bank", j, h][:],
                    lhsT=tiles["m_codes", j][:, block(g)].bitcast(FP8X4),
                    lhsT_scale=tiles["m_plane", j][:, block(g)],
                    rhs=w_codes[3, g, h][:].bitcast(FP8X4),
                    rhs_scale=w_plane[3, g, h][:],
                    start=(g == 0),
                    stop=(g == 1),
                )

        def round_y(j, h, source, copy):
            tiles["y_rounded", j, h] = work.tile([P, HALF], BF16, name="y_rounded", bufs=6)
            copy(
                out=tiles["y_rounded", j, h][:].rearrange("p (u m e) -> p u m e", u=2, e=2),
                in_=source.rearrange("p (m u e) -> p u m e", u=2, e=2),
            )

        def store_y(j):
            tiles["y", j] = work.tile([P, D], F32, name="y", bufs=4)
            for h in range(2):
                nc.scalar.copy(out=tiles["y", j][:, half(h)], in_=tiles["y_bank", j, h][:])
            nc.sync.dma_start(out=out_0[block(j), :], in_=tiles["y", j][:])

        def finish_last_y():
            j = TILES - 1
            tiles["y", j] = work.tile([P, D], F32, name="y", bufs=4)
            for h in range(2):
                round_y(j, h, tiles["y_bank", j, h][:], both_copies[h])
            for h in range(2):
                both_copies[h](out=tiles["y", j][:, half(h)], in_=tiles["y_bank", j, h][:])
                nc.sync.dma_start(out=out_0[block(j), half(h)], in_=tiles["y", j][:, half(h)])

        def turn_y(j, h):
            words = tiles["y_rounded", j, h][:].bitcast(F32)
            tiles["t_bank", j, h] = next_bank()
            for u in range(2):
                nc.tensor.transpose(tiles["t_bank", j, h][:, block(u)], words[:, block(u)], ident[:])

        def group_y(j, h, copy):
            tiles["y_grouped", j, h] = work.tile([P, HALF], BF16, name="y_grouped", bufs=4, align_bytes=64)
            copy(
                out=tiles["y_grouped", j, h][:].bitcast(F32).rearrange("p (r u) -> p r u", u=2),
                in_=tiles["t_bank", j, h][:, 0 : 2 * P].rearrange("p (u r) -> p r u", u=2),
            )

        y_plane = keep.tile([P, 2, T], U8, name="y_plane", align_bytes=64)

        def quantize_y(j):
            codes = work.tile([P, 2, P], U32, name="y_codes", bufs=4, align_bytes=64)
            for g in range(2):
                nc.vector.quantize_mx(
                    out=codes[:, g, :].bitcast(FP8X4), scales=y_plane[:, g, block(j)], in_=tiles["y_grouped", j, g][:]
                )
            nc.sync.dma_start(
                out=out_1[:, :, block(j), :].rearrange("g p m t -> p g (m t)").bitcast(I32), in_=codes[:].bitcast(I32)
            )

        both_copies = (nc.scalar.copy, nc.vector.tensor_copy)

        turn_x(0)
        group_x(0)
        turn_x(1)
        turn_guide()
        group_x(1)
        make_weights()
        quantize("x", 0)
        group_pieces(SCALAR_PIECES, nc.scalar.copy)
        quantize("x", 1)

        for step in range(TILES + PLANES_LAG):
            j1, j2, j3, jp = step, step - STAGE2_LAG, step - STAGE3_LAG, step - PLANES_LAG
            extra = 1 if step == 0 else 0
            if jp >= 0:
                turn_y(jp, 0)
                turn_y(jp, 1)
            if j1 < TILES:
                stage1(j1, 0)
                stage1(j1, 1)
                residual_and_weigh(j1, 0)
                residual_and_weigh(j1, 1)
            if 1 <= j1 <= TILES:
                turn_e(j1 - 1, 0)
                turn_e(j1 - 1, 1)
                keep_e(j1 - 1, 0)
                keep_e(j1 - 1, 1)
            if j1 + 2 < TILES:
                turn_x(j1 + 2)
                group_x(j1 + 2)
            if 0 <= j2 < TILES:
                stage2(j2, 0)
                stage2(j2, 1)
            if jp >= 0:
                group_y(jp, 0, nc.scalar.copy)
                group_y(jp, 1, both_copies[jp == TILES - 1])
            if 0 <= j3 < TILES:
                stage3(j3, 0)
                stage3(j3, 1)
            if 2 <= j1 + 1 < TILES:
                quantize("x", j1 + 1)
            if 0 <= j2 + 1 < TILES:
                quantize("e", j2 + 1)
            if 0 <= j2 < TILES:
                mix(j2)
            quantize_finished_chunks()
            group_pieces(VECTOR_PIECES + extra, nc.vector.tensor_copy)
            if 0 <= j2 + 2 < TILES:
                round_e(j2 + 2)
            if jp >= 0:
                quantize_y(jp)
            if 0 <= j3 < TILES - 1:
                store_y(j3)
            if j3 == TILES - 1:
                finish_last_y()
            group_pieces(SCALAR_PIECES + extra, nc.scalar.copy)
            if 0 <= j2 < TILES:
                quantize("m", j2)
            if 0 <= j3 < TILES - 1:
                round_y(j3, 0, tiles["y", j3][:, half(0)], nc.vector.tensor_copy)
                round_y(j3, 1, tiles["y", j3][:, half(1)], nc.vector.tensor_copy)

        for q in range(4):
            queue = nc.sync if q % 2 == 0 else nc.scalar
            queue.dma_start(
                out=out_2.bitcast(I32)[:, 4 * q : 4 * q + 4, :].rearrange("g r m -> r g m"),
                in_=y_plane[32 * q : 32 * q + 4, :, :].bitcast(I32),
            )
